import numpy as np, ml_dtypes
CORES = [5,13,21,29,133,141,149,157,261,389]
N = 10
COUNTS = [[0,0,100,25,0,0,0,12,0,0],[0,0,100,0,0,0,0,12,25,0],[25,25,0,12,25,12,25,25,0,25],[12,0,100,0,12,12,12,0,0,12],[25,25,100,0,0,12,0,0,12,25],[0,25,100,0,25,0,0,25,25,25],[0,0,100,12,0,25,0,12,0,12],[25,12,100,12,0,12,0,0,25,0],[12,0,100,12,25,12,12,12,0,25],[25,0,100,12,0,25,0,25,12,0]]
XW, YW = 225, 900
def setup_inputs(rng):
    return {"x": rng.standard_normal((N, 128, XW), dtype=np.float32).astype(ml_dtypes.bfloat16)}
def reference(x):
    y = np.full((N, 128, YW), np.nan, x.dtype)
    fill = [0] * N
    for s in range(N):
        o = 0
        for d in range(N):
            c = COUNTS[s][d]
            y[d][:, fill[d]:fill[d] + c] = x[s][:, o:o + c]
            o += c; fill[d] += c
    return {"y": y}

@@ -1,0 +1,123 @@
+SCRATCH = {
+    "xs": ("sbuf", [128, 225], "bfloat16"),
+    "land": ("sbuf", [128, 900], "bfloat16"),
+}
+SEMAPHORES = ["loaded", "sent", "near", "far", "stored", "in0", "in1"]
+
+OFF_CHIP, ON_CHIP, ENGINES = 0x00FF, 0xFF00, 8
+
+ROUTES = {
+    0: [(None, [(2, 100)]),
+        ((0, 0, 2), [(3, 25), (7, 12)])],
+    1: [((3, 1, 6), [(8, 25)]),
+        ((0, 1, 2), [(2, 100), (7, 12)])],
+    2: [((3, 2, 7), [(9, 25)]),
+        ((0, 2, 6), [(0, 25), (1, 25), (3, 12)]),
+        ((0, 2, 7), [(4, 25), (5, 12)]),
+        ((0, 2, 2), [(6, 25), (7, 25)])],
+    3: [((3, 3, 6), [(9, 12)]),
+        ((0, 3, 7), [(0, 12), (2, 44)]),
+        ((0, 3, 3), [(2, 56), (4, 12)]),
+        ((0, 3, 6), [(5, 12), (6, 12)])],
+    4: [((2, 0, 6), [(9, 25)]),
+        (None, [(2, 100)]),
+        ((1, 0, 6), [(0, 25), (1, 25)]),
+        ((1, 0, 7), [(5, 12), (8, 12)])],
+    5: [((0, 3, 6), [(2, 100)]),
+        ((2, 1, 6), [(8, 25), (9, 25)]),
+        (None, [(1, 25)]),
+        ((1, 1, 6), [(4, 25), (7, 25)])],
+    6: [((2, 2, 6), [(9, 12)]),
+        ((1, 2, 2), [(2, 100), (3, 12)]),
+        ((1, 2, 6), [(5, 25), (7, 12)])],
+    7: [((0, 3, 2), [(2, 100)]),
+        ((2, 3, 6), [(8, 25)]),
+        ((1, 3, 6), [(0, 25), (1, 12)]),
+        ((1, 3, 2), [(3, 12), (5, 12)])],
+    8: [((3, 2, 4), [(2, 50)]),
+        ((3, 2, 6), [(2, 50)]),
+        ((1, 0, 3), [(5, 12), (6, 12), (7, 12)]),
+        ((1, 0, 2), [(3, 12)]),
+        ((3, 0, 6), [(0, 12)]),
+        (None, [(9, 25)]),
+        ((2, 0, 0), [(4, 25)])],
+    9: [((3, 2, 0), [(2, 50)]),
+        ((3, 2, 2), [(2, 50)]),
+        ((0, 0, 3), [(3, 12), (5, 25), (7, 25)]),
+        (None, [(8, 12)]),
+        ((3, 0, 0), [(0, 25)])],
+}
+
+
+def _plan(cores, counts, topo):
+    n = len(cores)
+    wide = [sum(counts[s][d] for s in range(n)) > len(counts) * 25 for d in range(n)]
+    spans = {}
+    sends, owed = {}, {}
+    for s in range(n):
+        done = [0] * n
+        for via, blocks in ROUTES[s]:
+            x0 = sum(counts[s][:blocks[0][0]]) + done[blocks[0][0]]
+            out, at = [], x0
+            for d, w in blocks:
+                assert at == sum(counts[s][:d]) + done[d]
+                far = wide[d] and topo.rack(topo.host(cores[s])) != topo.rack(topo.host(cores[d]))
+                out.append((d, sum(counts[t][d] for t in range(s)) + done[d], w, "far" if far else "near"))
+                done[d] += w
+                at += w
+            if via is None:
+                d, y0, w, sem = out[0]
+                sends.setdefault(cores[s], []).append((None, cores[d], "xs", x0, y0, w, sem))
+                owed.setdefault(cores[d], {}).setdefault(sem, 0)
+                owed[cores[d]][sem] += ENGINES
+            else:
+                helper = via[0] * 128 + via[1] * 8 + via[2]
+                spans.setdefault(helper, []).append((at - x0, cores[s], x0, out))
+                sends.setdefault(cores[s], []).append([None, helper, "xs", x0, None, at - x0, None])
+        assert done == list(counts[s])
+    for helper, got in spans.items():
+        col = 0
+        for k, (width, src, x0, out) in enumerate(sorted(got, key=lambda t: -t[0])):
+            for w in sends[src]:
+                if w[1] == helper and w[3] == x0:
+                    w[4], w[6] = col, "in%d" % k
+            for d, y0, w, sem in out:
+                sends.setdefault(helper, []).append(("in%d" % k, cores[d], "land", col, y0, w, sem))
+                owed.setdefault(cores[d], {}).setdefault(sem, 0)
+                owed[cores[d]][sem] += ENGINES
+                col += w
+    return sends, owed
+
+
+def rank_program(g, core, T, topo):
+    counts = T.tables["COUNTS"]
+    sends, owed = _plan(T.cores, counts, topo)
+    rank = T.rank_of(core)
+    if core not in sends:
+        return
+    if rank is not None:
+        used = sum(counts[rank])
+        g.sync.dma_start(T.xs[:, 0:used], T.x[:, 0:used]).then_inc(T.sem.loaded, 16)
+        g.wait_ge(T.sem.loaded, 16)
+    waited = None
+    for trigger, dst, buf, c0, c1, w, sem in sends[core]:
+        if trigger is not None and trigger != waited:
+            g.wait_ge(T.sem[trigger], ENGINES)
+            waited = trigger
+        rid, pid = topo.addr(dst, core)
+        on_chip = dst // 8 == core // 8
+        g.remote_dma(T.land[:, c1:c1 + w], T[buf][:, c0:c0 + w], T.sem[sem], T.sem.sent, pid, rid,
+                     ON_CHIP if on_chip else OFF_CHIP)
+    if rank is not None:
+        n = len(T.cores)
+        total = sum(counts[s][rank] for s in range(n))
+        cut = total
+        if "far" in owed[core]:
+            mine = topo.rack(topo.host(core))
+            cut = sum(counts[s][rank] for s in range(n) if topo.rack(topo.host(T.cores[s])) == mine)
+            g.scalar.wait_ge(T.sem.far, owed[core]["far"])
+            g.scalar.dma_start(T.y[:, cut:total], T.land[:, cut:total]).then_inc(T.sem.stored, 16)
+        g.sync.wait_ge(T.sem.near, owed[core]["near"])
+        g.sync.dma_start(T.y[:, 0:cut], T.land[:, 0:cut]).then_inc(T.sem.stored, 16)
+        g.wait_ge(T.sem.stored, 32 if cut < total else 16)
+    g.wait_ge(T.sem.sent, ENGINES * len(sends[core]))

@@ -1,10 +1,13 @@
+from concourse.bass import DstId, RemoteDMATransfer
+
 SCRATCH = {
     "xs": ("sbuf", [128, 225], "bfloat16"),
     "land": ("sbuf", [128, 900], "bfloat16"),
 }
-SEMAPHORES = ["loaded", "sent", "near", "far", "stored", "in0", "in1"]
+SEMAPHORES = ["loaded", "got", "near", "far", "sent", "stored"]
 
-OFF_CHIP, ON_CHIP, ENGINES = 0x00FF, 0xFF00, 8
+OFF_CHIP = {1: (0x00FF,), 2: (0x000F, 0x00F0)}
+ON_CHIP = {1: (0xFF00,), 2: (0x0F00, 0xF000)}
 
 ROUTES = {
     0: [(None, [(2, 100)]),
@@ -15,20 +18,22 @@ ROUTES = {
         ((0, 2, 6), [(0, 25), (1, 25), (3, 12)]),
         ((0, 2, 7), [(4, 25), (5, 12)]),
         ((0, 2, 2), [(6, 25), (7, 25)])],
-    3: [((3, 3, 6), [(9, 12)]),
-        ((0, 3, 7), [(0, 12), (2, 44)]),
-        ((0, 3, 3), [(2, 56), (4, 12)]),
-        ((0, 3, 6), [(5, 12), (6, 12)])],
-    4: [((2, 0, 6), [(9, 25)]),
-        (None, [(2, 100)]),
+    3: [((0, 3, 7), [(2, 50)]),
+        ((0, 3, 3), [(2, 50)]),
+        ((3, 3, 6), [(9, 12)]),
+        ((0, 1, 6), [(0, 12)]),
+        ((1, 3, 7), [(6, 12)]),
+        ((1, 1, 7), [(4, 12), (5, 12)])],
+    4: [(None, [(2, 100)]),
+        ((2, 0, 6), [(9, 25)]),
         ((1, 0, 6), [(0, 25), (1, 25)]),
         ((1, 0, 7), [(5, 12), (8, 12)])],
     5: [((0, 3, 6), [(2, 100)]),
         ((2, 1, 6), [(8, 25), (9, 25)]),
-        (None, [(1, 25)]),
-        ((1, 1, 6), [(4, 25), (7, 25)])],
-    6: [((2, 2, 6), [(9, 12)]),
-        ((1, 2, 2), [(2, 100), (3, 12)]),
+        ((1, 1, 6), [(4, 25), (7, 25)]),
+        (None, [(1, 25)])],
+    6: [((1, 2, 2), [(2, 100), (3, 12)]),
+        ((2, 2, 6), [(9, 12)]),
         ((1, 2, 6), [(5, 25), (7, 12)])],
     7: [((0, 3, 2), [(2, 100)]),
         ((2, 3, 6), [(8, 25)]),
@@ -38,7 +43,7 @@ ROUTES = {
         ((3, 2, 6), [(2, 50)]),
         ((1, 0, 3), [(5, 12), (6, 12), (7, 12)]),
         ((1, 0, 2), [(3, 12)]),
-        ((3, 0, 6), [(0, 12)]),
+        ((1, 0, 0), [(0, 12)]),
         (None, [(9, 25)]),
         ((2, 0, 0), [(4, 25)])],
     9: [((3, 2, 0), [(2, 50)]),
@@ -49,75 +54,88 @@ ROUTES = {
 }
 
 
-def _plan(cores, counts, topo):
+def _bits(mask):
+    return bin(mask).count("1")
+
+
+def _plan(cores, counts, xw, topo):
     n = len(cores)
-    wide = [sum(counts[s][d] for s in range(n)) > len(counts) * 25 for d in range(n)]
-    spans = {}
-    sends, owed = {}, {}
+    rack = [topo.rack(topo.host(c)) for c in cores]
+    total = [sum(counts[s][d] for s in range(n)) for d in range(n)]
+    writes = {}
     for s in range(n):
         done = [0] * n
         for via, blocks in ROUTES[s]:
-            x0 = sum(counts[s][:blocks[0][0]]) + done[blocks[0][0]]
-            out, at = [], x0
+            x0 = col = sum(counts[s][:blocks[0][0]]) + done[blocks[0][0]]
+            src, buf, base = cores[s], "xs", x0
+            if via is not None:
+                src, buf, base = via[0] * 128 + via[1] * 8 + via[2], "land", 0
+                assert src not in writes and src not in cores
+                writes.setdefault(cores[s], []).append((src, "xs", x0, 0, sum(w for _, w in blocks), "got"))
             for d, w in blocks:
-                assert at == sum(counts[s][:d]) + done[d]
-                far = wide[d] and topo.rack(topo.host(cores[s])) != topo.rack(topo.host(cores[d]))
-                out.append((d, sum(counts[t][d] for t in range(s)) + done[d], w, "far" if far else "near"))
+                assert col == sum(counts[s][:d]) + done[d]
+                y0 = sum(counts[t][d] for t in range(s)) + done[d]
+                sem = "far" if total[d] > xw and rack[s] != rack[d] else "near"
+                writes.setdefault(src, []).append((cores[d], buf, base + col - x0, y0, w, sem))
                 done[d] += w
-                at += w
-            if via is None:
-                d, y0, w, sem = out[0]
-                sends.setdefault(cores[s], []).append((None, cores[d], "xs", x0, y0, w, sem))
-                owed.setdefault(cores[d], {}).setdefault(sem, 0)
-                owed[cores[d]][sem] += ENGINES
-            else:
-                helper = via[0] * 128 + via[1] * 8 + via[2]
-                spans.setdefault(helper, []).append((at - x0, cores[s], x0, out))
-                sends.setdefault(cores[s], []).append([None, helper, "xs", x0, None, at - x0, None])
-        assert done == list(counts[s])
-    for helper, got in spans.items():
-        col = 0
-        for k, (width, src, x0, out) in enumerate(sorted(got, key=lambda t: -t[0])):
-            for w in sends[src]:
-                if w[1] == helper and w[3] == x0:
-                    w[4], w[6] = col, "in%d" % k
-            for d, y0, w, sem in out:
-                sends.setdefault(helper, []).append(("in%d" % k, cores[d], "land", col, y0, w, sem))
-                owed.setdefault(cores[d], {}).setdefault(sem, 0)
-                owed[cores[d]][sem] += ENGINES
                 col += w
-    return sends, owed
+        assert done == list(counts[s])
+    calls, owed = {}, {}
+    for core, ws in writes.items():
+        calls[core] = []
+        widths = []
+        for wr in ws:
+            if wr[4] not in widths:
+                widths.append(wr[4])
+        for width in widths:
+            off = [wr for wr in ws if wr[4] == width and wr[0] // 8 != core // 8]
+            on = [wr for wr in ws if wr[4] == width and wr[0] // 8 == core // 8]
+            while off or on:
+                call = []
+                for some, masks in ((off[:2], OFF_CHIP), (on[:2], ON_CHIP)):
+                    for i, wr in enumerate(some):
+                        mask = masks[len(some)][i]
+                        call.append(wr + (mask,))
+                        at = owed.setdefault(wr[0], {})
+                        at[wr[5]] = at.get(wr[5], 0) + _bits(mask)
+                calls[core].append(call)
+                off, on = off[2:], on[2:]
+    return calls, owed
 
 
 def rank_program(g, core, T, topo):
     counts = T.tables["COUNTS"]
-    sends, owed = _plan(T.cores, counts, topo)
-    rank = T.rank_of(core)
-    if core not in sends:
+    calls, owed = _plan(T.cores, counts, T.tables["XW"], topo)
+    if core not in calls:
         return
+    rank = T.rank_of(core)
     if rank is not None:
         used = sum(counts[rank])
         g.sync.dma_start(T.xs[:, 0:used], T.x[:, 0:used]).then_inc(T.sem.loaded, 16)
         g.wait_ge(T.sem.loaded, 16)
-    waited = None
-    for trigger, dst, buf, c0, c1, w, sem in sends[core]:
-        if trigger is not None and trigger != waited:
-            g.wait_ge(T.sem[trigger], ENGINES)
-            waited = trigger
-        rid, pid = topo.addr(dst, core)
-        on_chip = dst // 8 == core // 8
-        g.remote_dma(T.land[:, c1:c1 + w], T[buf][:, c0:c0 + w], T.sem[sem], T.sem.sent, pid, rid,
-                     ON_CHIP if on_chip else OFF_CHIP)
+    else:
+        g.wait_ge(T.sem.got, owed[core]["got"])
+    sent = 0
+    for call in calls[core]:
+        transfers = []
+        for dst, buf, c0, c1, w, sem, mask in call:
+            rid, pid = topo.addr(dst, core)
+            transfers.append(RemoteDMATransfer(dst_ids=[DstId(rid=rid, pnc=pid)], dma_engine_mask=mask,
+                                               remote_sem=T.sem[sem], src=T[buf][:, c0:c0 + w], dst=T.land[:, c1:c1 + w]))
+            sent += _bits(mask)
+        g.remote_dma_fused(transfers, local_sem=T.sem.sent)
     if rank is not None:
         n = len(T.cores)
         total = sum(counts[s][rank] for s in range(n))
         cut = total
         if "far" in owed[core]:
-            mine = topo.rack(topo.host(core))
-            cut = sum(counts[s][rank] for s in range(n) if topo.rack(topo.host(T.cores[s])) == mine)
+            home = topo.rack(topo.host(core))
+            away = [topo.rack(topo.host(c)) != home for c in T.cores]
+            assert away == sorted(away)
+            cut = sum(counts[s][rank] for s in range(n) if not away[s])
             g.scalar.wait_ge(T.sem.far, owed[core]["far"])
             g.scalar.dma_start(T.y[:, cut:total], T.land[:, cut:total]).then_inc(T.sem.stored, 16)
         g.sync.wait_ge(T.sem.near, owed[core]["near"])
         g.sync.dma_start(T.y[:, 0:cut], T.land[:, 0:cut]).then_inc(T.sem.stored, 16)
         g.wait_ge(T.sem.stored, 32 if cut < total else 16)
-    g.wait_ge(T.sem.sent, ENGINES * len(sends[core]))
+    g.wait_ge(T.sem.sent, sent)

from concourse.bass import DstId, RemoteDMATransfer

SCRATCH = {
    "xs": ("sbuf", [128, 225], "bfloat16"),
    "land": ("sbuf", [128, 900], "bfloat16"),
}
SEMAPHORES = ["loaded", "got", "near", "far", "sent", "stored"]

OFF_CHIP = {1: (0x00FF,), 2: (0x000F, 0x00F0)}
ON_CHIP = {1: (0xFF00,), 2: (0x0F00, 0xF000)}

ROUTES = {
    0: [(None, [(2, 100)]),
        ((0, 0, 2), [(3, 25), (7, 12)])],
    1: [((3, 1, 6), [(8, 25)]),
        ((0, 1, 2), [(2, 100), (7, 12)])],
    2: [((3, 2, 7), [(9, 25)]),
        ((0, 2, 6), [(0, 25), (1, 25), (3, 12)]),
        ((0, 2, 7), [(4, 25), (5, 12)]),
        ((0, 2, 2), [(6, 25), (7, 25)])],
    3: [((0, 3, 7), [(2, 50)]),
        ((0, 3, 3), [(2, 50)]),
        ((3, 3, 6), [(9, 12)]),
        ((0, 1, 6), [(0, 12)]),
        ((1, 3, 7), [(6, 12)]),
        ((1, 1, 7), [(4, 12), (5, 12)])],
    4: [(None, [(2, 100)]),
        ((2, 0, 6), [(9, 25)]),
        ((1, 0, 6), [(0, 25), (1, 25)]),
        ((1, 0, 7), [(5, 12), (8, 12)])],
    5: [((0, 3, 6), [(2, 100)]),
        ((2, 1, 6), [(8, 25), (9, 25)]),
        ((1, 1, 6), [(4, 25), (7, 25)]),
        (None, [(1, 25)])],
    6: [((1, 2, 2), [(2, 100), (3, 12)]),
        ((2, 2, 6), [(9, 12)]),
        ((1, 2, 6), [(5, 25), (7, 12)])],
    7: [((0, 3, 2), [(2, 100)]),
        ((2, 3, 6), [(8, 25)]),
        ((1, 3, 6), [(0, 25), (1, 12)]),
        ((1, 3, 2), [(3, 12), (5, 12)])],
    8: [((3, 2, 4), [(2, 50)]),
        ((3, 2, 6), [(2, 50)]),
        ((1, 0, 3), [(5, 12), (6, 12), (7, 12)]),
        ((1, 0, 2), [(3, 12)]),
        ((1, 0, 0), [(0, 12)]),
        (None, [(9, 25)]),
        ((2, 0, 0), [(4, 25)])],
    9: [((3, 2, 0), [(2, 50)]),
        ((3, 2, 2), [(2, 50)]),
        ((0, 0, 3), [(3, 12), (5, 25), (7, 25)]),
        (None, [(8, 12)]),
        ((3, 0, 0), [(0, 25)])],
}


def _bits(mask):
    return bin(mask).count("1")


def _plan(cores, counts, xw, topo):
    n = len(cores)
    rack = [topo.rack(topo.host(c)) for c in cores]
    total = [sum(counts[s][d] for s in range(n)) for d in range(n)]
    writes = {}
    for s in range(n):
        done = [0] * n
        for via, blocks in ROUTES[s]:
            x0 = col = sum(counts[s][:blocks[0][0]]) + done[blocks[0][0]]
            src, buf, base = cores[s], "xs", x0
            if via is not None:
                src, buf, base = via[0] * 128 + via[1] * 8 + via[2], "land", 0
                assert src not in writes and src not in cores
                writes.setdefault(cores[s], []).append((src, "xs", x0, 0, sum(w for _, w in blocks), "got"))
            for d, w in blocks:
                assert col == sum(counts[s][:d]) + done[d]
                y0 = sum(counts[t][d] for t in range(s)) + done[d]
                sem = "far" if total[d] > xw and rack[s] != rack[d] else "near"
                writes.setdefault(src, []).append((cores[d], buf, base + col - x0, y0, w, sem))
                done[d] += w
                col += w
        assert done == list(counts[s])
    calls, owed = {}, {}
    for core, ws in writes.items():
        calls[core] = []
        widths = []
        for wr in ws:
            if wr[4] not in widths:
                widths.append(wr[4])
        for width in widths:
            off = [wr for wr in ws if wr[4] == width and wr[0] // 8 != core // 8]
            on = [wr for wr in ws if wr[4] == width and wr[0] // 8 == core // 8]
            while off or on:
                call = []
                for some, masks in ((off[:2], OFF_CHIP), (on[:2], ON_CHIP)):
                    for i, wr in enumerate(some):
                        mask = masks[len(some)][i]
                        call.append(wr + (mask,))
                        at = owed.setdefault(wr[0], {})
                        at[wr[5]] = at.get(wr[5], 0) + _bits(mask)
                calls[core].append(call)
                off, on = off[2:], on[2:]
    return calls, owed


def rank_program(g, core, T, topo):
    counts = T.tables["COUNTS"]
    calls, owed = _plan(T.cores, counts, T.tables["XW"], topo)
    if core not in calls:
        return
    rank = T.rank_of(core)
    if rank is not None:
        used = sum(counts[rank])
        g.sync.dma_start(T.xs[:, 0:used], T.x[:, 0:used]).then_inc(T.sem.loaded, 16)
        g.wait_ge(T.sem.loaded, 16)
    else:
        g.wait_ge(T.sem.got, owed[core]["got"])
    sent = 0
    for call in calls[core]:
        transfers = []
        for dst, buf, c0, c1, w, sem, mask in call:
            rid, pid = topo.addr(dst, core)
            transfers.append(RemoteDMATransfer(dst_ids=[DstId(rid=rid, pnc=pid)], dma_engine_mask=mask,
                                               remote_sem=T.sem[sem], src=T[buf][:, c0:c0 + w], dst=T.land[:, c1:c1 + w]))
            sent += _bits(mask)
        g.remote_dma_fused(transfers, local_sem=T.sem.sent)
    if rank is not None:
        n = len(T.cores)
        total = sum(counts[s][rank] for s in range(n))
        cut = total
        if "far" in owed[core]:
            home = topo.rack(topo.host(core))
            away = [topo.rack(topo.host(c)) != home for c in T.cores]
            assert away == sorted(away)
            cut = sum(counts[s][rank] for s in range(n) if not away[s])
            g.scalar.wait_ge(T.sem.far, owed[core]["far"])
            g.scalar.dma_start(T.y[:, cut:total], T.land[:, cut:total]).then_inc(T.sem.stored, 16)
        g.sync.wait_ge(T.sem.near, owed[core]["near"])
        g.sync.dma_start(T.y[:, 0:cut], T.land[:, 0:cut]).then_inc(T.sem.stored, 16)
        g.wait_ge(T.sem.stored, 32 if cut < total else 16)
    g.wait_ge(T.sem.sent, sent)
